import numpy as np
import ml_dtypes


def mxq(x, axis, fmt="e4m3"):
    dtype, down = {"e4m3": (ml_dtypes.float8_e4m3fn, 7), "e5m2": (ml_dtypes.float8_e5m2, 14)}[fmt]
    v = np.moveaxis(np.asarray(x, np.float32).astype(ml_dtypes.bfloat16).astype(np.float64), axis, -1)
    blocks = v.reshape(v.shape[:-1] + (-1, 32))
    amax = np.abs(blocks).max(-1, keepdims=True)
    byte = np.maximum(np.where(amax > 0, np.frexp(amax)[1] - 1 + 127, 0) - down, 1)
    scale = np.exp2(byte - 127.0)
    codes = (blocks / scale).astype(np.float32).astype(dtype).astype(np.float64)
    return np.moveaxis((codes * scale).reshape(v.shape), -1, axis)


WIDE = False


def mx_kscale(k):
    if not WIDE:
        return np.ones(k)
    levels = np.array([30, -30])
    if k % 512:
        return np.exp2(np.random.permutation(np.resize(levels, k // 32))).repeat(32)
    a = np.empty((k // 512, 16))
    for p in range(k // 512):
        a[p, :8] = np.random.permutation(np.resize(levels, 8))
        for g in range(8):
            far = levels[np.abs(levels - a[p, g]) >= 10]
            a[p, g + 8] = far[np.random.randint(len(far))]
    return np.exp2(a.ravel()).repeat(32)


def f64(x):
    return np.asarray(x).astype(np.float64)


def striped(idx):
    return np.tile(np.asarray(idx).reshape(-1, 16).T, (8, 1)).astype(np.uint16)


def unstriped(offs):
    return offs[:16].T.reshape(-1).astype(np.int64)


def striped8(idx):
    return np.asarray(idx).reshape(8, -1, 16).transpose(0, 2, 1).reshape(128, -1).astype(np.uint16)


def unstriped8(offs):
    return offs.reshape(8, 16, -1).transpose(0, 2, 1).reshape(8, -1).astype(np.int64)


def pick8(x, idx, run):
    r = np.arange(len(x))
    return x[r[:, None], idx[r % (8 * run) // run]]


E2M1 = np.array([0.0, 0.5, 1.0, 1.5, 2.0, 3.0, 4.0, 6.0, -0.0, -0.5, -1.0, -1.5, -2.0, -3.0, -4.0, -6.0])


def pack_weight(w, fmt):
    k, n = w.shape
    w = f64(np.asarray(w, np.float32).astype(ml_dtypes.bfloat16)).reshape(k // 32, 32, n)
    amax = np.abs(w).max(1)
    if fmt in ("e4m3", "e5m2"):
        byte = np.frexp(amax)[1] - 1 + 127 - (7 if fmt == "e4m3" else 14)
    else:
        mant, ex = np.frexp(amax / 6.0)
        byte = np.where(mant > 0.5, ex, ex - 1) + 127
    byte = np.clip(np.where(amax > 0, byte, 1), 1, 254)
    scaled = (w * np.exp2(127.0 - byte)[:, None, :]).reshape(k, n).astype(np.float32)
    by_word = np.ascontiguousarray(scaled.reshape(k // 512, 128, 4, n).transpose(0, 1, 3, 2))
    if fmt in ("e4m3", "e5m2"):
        words = by_word.astype(ml_dtypes.float8_e4m3fn if fmt == "e4m3" else ml_dtypes.float8_e5m2).view(np.uint8)
    else:
        c = by_word.astype(ml_dtypes.float4_e2m1fn).view(np.uint8) & 0xF
        words = (c[..., 0::2] | (c[..., 1::2] << 4)).reshape(k // 512, 128, 2 * n)
    return np.ascontiguousarray(words), np.ascontiguousarray(byte.astype(np.uint8).reshape(k // 512, 16, n))


def unpack_weight(words, scales, fmt):
    g, _, n = scales.shape
    words = np.ascontiguousarray(words).reshape(g, 128, n, -1)
    if fmt in ("e4m3", "e5m2"):
        vals = words.view(ml_dtypes.float8_e4m3fn if fmt == "e4m3" else ml_dtypes.float8_e5m2).astype(np.float64)
    else:
        nib = np.empty((g, 128, n, 4), np.uint8)
        nib[..., 0::2] = words & 0xF
        nib[..., 1::2] = words >> 4
        vals = E2M1[nib]
    vals = vals * np.repeat(np.exp2(scales.astype(np.float64) - 127.0), 8, axis=1)[..., None]
    return vals.transpose(0, 1, 3, 2).reshape(g * 512, n)


def sgn(shape):
    return np.random.uniform(0.5, 2.0, shape) * np.where(np.random.standard_normal(shape) < 0, -1.0, 1.0)


K, T, J, R, V, C, O, N, E = 512, 1024, 256, 512, 1024, 512, 256, 256, 1024


def setup_inputs():
    n = np.random.standard_normal
    idx = np.random.permutation(V)[:R]
    idx2 = np.random.permutation(T)[:J]
    idx3 = np.stack([np.random.permutation(C)[:J] for _ in range(8)])
    idx4 = np.random.permutation(C)[:C]
    idx5 = np.random.permutation(C)[:O]
    idx6 = np.random.permutation(T)[:O]
    idx7 = np.random.permutation(E)[:O]
    fk = mx_kscale(K)
    fr = mx_kscale(R)
    tr = np.ones(V)
    tr[idx] = fr
    xtp = pack_weight(n((K, T)) / fk[:, None], "e2m1")
    wtp = pack_weight(n((K, V)) * 1 / np.sqrt(K) * fk[:, None] * tr, "e5m2")
    wbp = pack_weight(n((R, N)) * 1 / np.sqrt(R) / fr[:, None], "e4m3")
    wsp = pack_weight(n((K, N)) * 1 / np.sqrt(K) * fk[:, None], "e4m3")
    return {
        "xt_words": xtp[0],
        "xt_scales": xtp[1],
        "wt_words": wtp[0],
        "wt_scales": wtp[1],
        "sa": (sgn((R, 1))).astype(np.float32),
        "wb_words": wbp[0],
        "wb_scales": wbp[1],
        "ws_words": wsp[0],
        "ws_scales": wsp[1],
        "offs": striped(idx),
        "offs2": striped(idx2),
        "offs3": striped8(idx3),
        "offs4": striped(idx4),
        "offs5": striped(idx5),
        "offs6": striped(idx6),
        "offs7": striped(idx7),
    }


def reference(xt_words, xt_scales, wt_words, wt_scales, sa, wb_words, wb_scales, ws_words, ws_scales, offs, offs2, offs3, offs4, offs5, offs6, offs7):
    idx = unstriped(offs)
    idx2 = unstriped(offs2)
    idx3 = unstriped8(offs3)
    idx4 = unstriped(offs4)
    idx5 = unstriped(offs5)
    idx6 = unstriped(offs6)
    idx7 = unstriped(offs7)
    xtu = unpack_weight(xt_words, xt_scales, "e2m1")
    wtu = unpack_weight(wt_words, wt_scales, "e5m2")
    wbu = unpack_weight(wb_words, wb_scales, "e4m3")
    wsu = unpack_weight(ws_words, ws_scales, "e4m3")
    wtidxg = wtu[:, idx]
    xtidx2g = xtu[:, idx2]
    a = wtidxg.T @ xtidx2g
    pw = np.zeros((R, C))
    pw[np.arange(R)[:, None], idx3[np.arange(R) % 512 // 64]] = a
    pg = np.maximum(pw, pw[:, idx4] * f64(sa))
    hid = pg[:, idx5]
    hidq = mxq(hid, 0, "e5m2")
    xtidx6g = xtu[:, idx6]
    p = wbu.T @ hidq + wsu.T @ xtidx6g
    y = np.zeros((N, E))
    y[:, idx7] = p
    return y

@@ -1,0 +1,206 @@
+from contextlib import ExitStack
+
+import concourse.mybir as mybir
+
+K, T, J, R, V, C, O, N, E = 512, 1024, 256, 512, 1024, 512, 256, 256, 1024
+FLOPS = 2 * K * R * J + 2 * R * N * O + 2 * K * N * O
+
+F32 = mybir.dt.float32
+BF16 = mybir.dt.bfloat16
+I32 = mybir.dt.int32
+U32 = mybir.dt.uint32
+U16 = mybir.dt.uint16
+U8 = mybir.dt.uint8
+E4M3 = mybir.dt.float8_e4m3fn_x4
+E5M2 = mybir.dt.float8_e5m2_x4
+E2M1 = mybir.dt.float4_e2m1fn_x4
+COPY = mybir.ActivationFunctionType.Copy
+MAX = mybir.AluOpType.max
+
+P = 128
+PACK = 4
+HALF = C // 2
+
+
+def load_scale_rows(queue, plane, scales):
+    for q in range(4):
+        queue.dma_start(
+            out=plane[32 * q : 32 * q + 4, :].bitcast(I32),
+            in_=scales[0, 4 * q : 4 * q + 4, :].bitcast(I32),
+        )
+
+
+def tile_list_ownladder_chosen_further_scattered_kernel(
+    tc, xt_words, xt_scales, wt_words, wt_scales, sa, wb_words, wb_scales, ws_words, ws_scales,
+    offs, offs2, offs3, offs4, offs5, offs6, offs7, out,
+):
+    nc = tc.nc
+    with ExitStack() as ctx:
+        lists = ctx.enter_context(tc.tile_pool(name="lists", bufs=1))
+        keep = ctx.enter_context(tc.tile_pool(name="keep", bufs=1))
+        psum = ctx.enter_context(tc.psum_pool(name="psum", bufs=1))
+
+        def list_tile(name, entries):
+            return lists.tile([P, entries // 16], U16, name=name)
+
+        l1 = list_tile("l1", R)
+        l2 = list_tile("l2", J)
+        l3 = list_tile("l3", J)
+        l4 = list_tile("l4", C)
+        l5 = list_tile("l5", O)
+        l6 = list_tile("l6", O)
+        l7 = list_tile("l7", O)
+
+        wt_w = keep.tile([P, V], U32, name="wt_w", align_bytes=64)
+        wt_s = keep.tile([P, V], U8, name="wt_s", align_bytes=64)
+        xt_w = keep.tile([P, T], U16, name="xt_w", align_bytes=64)
+        xt_s = keep.tile([P, T], U8, name="xt_s", align_bytes=64)
+        wb_w = keep.tile([P, N], U32, name="wb_w", align_bytes=64)
+        wb_s = keep.tile([P, N], U8, name="wb_s", align_bytes=64)
+        ws_w = keep.tile([P, N], U32, name="ws_w", align_bytes=64)
+        ws_s = keep.tile([P, N], U8, name="ws_s", align_bytes=64)
+        sa_t = keep.tile([P, PACK], F32, name="sa_t")
+        pw = [keep.tile([P, C], F32, name="pw%d" % t) for t in range(PACK)]
+
+        nc.vector.memset(wt_s[:].bitcast(I32), 0)
+        nc.vector.memset(xt_s[:].bitcast(I32), 0)
+        nc.vector.memset(ws_s[:].bitcast(I32), 0)
+        nc.vector.memset(wb_s[:].bitcast(I32), 0)
+        for t in range(PACK):
+            nc.vector.memset(pw[t][:], 0.0)
+
+        nc.sync.dma_start(l1[:], offs)
+        load_scale_rows(nc.scalar, wt_s, wt_scales)
+        nc.sync.dma_start(out=xt_w[:].bitcast(I32), in_=xt_words[0].bitcast(I32))
+        nc.sync.dma_start(l2[:], offs2)
+        nc.sync.dma_start(
+            out=wt_w[:].bitcast(I32), in_=wt_words[0].rearrange("p n t -> p (n t)").bitcast(I32)
+        )
+        load_scale_rows(nc.scalar, xt_s, xt_scales)
+        nc.sync.dma_start(l3[:], offs3)
+        nc.sync.dma_start(out=sa_t[:], in_=sa.rearrange("(p t) o -> p (t o)", t=PACK))
+        nc.sync.dma_start(l4[:], offs4)
+        nc.sync.dma_start(l6[:], offs6)
+        nc.sync.dma_start(l5[:], offs5)
+        nc.sync.dma_start(
+            out=ws_w[:].bitcast(I32), in_=ws_words[0].rearrange("p n t -> p (n t)").bitcast(I32)
+        )
+        load_scale_rows(nc.sync, ws_s, ws_scales)
+        nc.sync.dma_start(
+            out=wb_w[:].bitcast(I32), in_=wb_words[0].rearrange("p n t -> p (n t)").bitcast(I32)
+        )
+        load_scale_rows(nc.sync, wb_s, wb_scales)
+        nc.sync.dma_start(l7[:], offs7)
+
+        g_ws = keep.tile([P, PACK, P], U8, name="g_ws", align_bytes=64)
+        g_ww = keep.tile([P, PACK, P], U32, name="g_ww", align_bytes=64)
+        x2_w = keep.tile([P, J], U16, name="x2_w", align_bytes=64)
+        x2_s = keep.tile([P, J], U8, name="x2_s", align_bytes=64)
+        nc.vector.tensor_copy(g_ws[:].rearrange("p t m -> p m t"), wt_s[:].indirect(l1[:]))
+        nc.vector.tensor_copy(x2_w[:], xt_w[:].indirect(l2[:]))
+        nc.vector.tensor_copy(g_ww[:].rearrange("p t m -> p m t"), wt_w[:].indirect(l1[:]))
+        nc.vector.tensor_copy(x2_s[:], xt_s[:].indirect(l2[:]))
+
+        a_sb = []
+        for t in range(PACK):
+            acc = psum.tile([P, J], F32, name="a_ps%d" % t)
+            nc.tensor.matmul_mx(
+                out=acc[:],
+                lhsT=g_ww[:, t, :].bitcast(E5M2),
+                lhsT_scale=g_ws[:, t, :],
+                rhs=x2_w[:].bitcast(E2M1),
+                rhs_scale=x2_s[:],
+                start=True,
+                stop=True,
+            )
+            a_t = keep.tile([P, J], F32, name="a_sb%d" % t, tag="slot%d" % t)
+            if t == 0:
+                nc.scalar.copy(a_t[:], acc[:])
+            else:
+                nc.vector.tensor_copy(a_t[:], acc[:])
+            a_sb.append(a_t)
+
+        x6_w = keep.tile([P, O], U16, name="x6_w", align_bytes=64)
+        x6_s = keep.tile([P, O], U8, name="x6_s", align_bytes=64)
+        nc.vector.tensor_copy(x6_w[:], xt_w[:].indirect(l6[:]))
+        nc.vector.tensor_copy(x6_s[:], xt_s[:].indirect(l6[:]))
+        p_ps = [psum.tile([P, O], F32, name="p_ps%d" % h) for h in range(2)]
+        for h in range(2):
+            cols = slice(h * P, (h + 1) * P)
+            nc.tensor.matmul_mx(
+                out=p_ps[h][:],
+                lhsT=ws_w[:, cols].bitcast(E4M3),
+                lhsT_scale=ws_s[:, cols],
+                rhs=x6_w[:].bitcast(E2M1),
+                rhs_scale=x6_s[:],
+                start=True,
+                stop=False,
+            )
+
+        hid = keep.tile([P, O, PACK], BF16, name="hid", align_bytes=64)
+        looked = [keep.tile([P, C], F32, name="looked%d" % t) for t in range(PACK)]
+        pg = [keep.tile([P, C], F32, name="pg%d" % t) for t in range(PACK)]
+
+        def place(t):
+            nc.scalar.activation(pw[t][:].indirect(l3[:]), a_sb[t][:], COPY)
+
+        def look(t, u):
+            cols = slice(u * HALF, (u + 1) * HALF)
+            entries = slice(u * HALF // 16, (u + 1) * HALF // 16)
+            nc.scalar.activation(
+                looked[t][:, cols], pw[t][:].indirect(l4[:, entries]), COPY, scale=sa_t[:, t : t + 1]
+            )
+            nc.vector.tensor_tensor(pg[t][:, cols], pw[t][:, cols], looked[t][:, cols], MAX)
+
+        def pick(t):
+            nc.vector.tensor_copy(hid[:, :, t], pg[t][:].indirect(l5[:]))
+
+        pages = []
+
+        def clear_page(h):
+            page = keep.tile([P, E], F32, name="page%d" % h, tag="slot%d" % h)
+            nc.vector.memset(page[:], 0.0)
+            pages.append(page)
+
+        place(0)
+        place(1)
+        look(0, 0)
+        look(0, 1)
+        pick(0)
+        clear_page(0)
+        place(2)
+        look(1, 0)
+        look(1, 1)
+        pick(1)
+        clear_page(1)
+        look(2, 0)
+        place(3)
+        look(2, 1)
+        pick(2)
+        look(3, 0)
+        look(3, 1)
+        pick(3)
+
+        h_w = keep.tile([P, O], U32, name="h_w", align_bytes=64)
+        h_s = keep.tile([P, O], U8, name="h_s", align_bytes=64)
+        nc.vector.quantize_mx(
+            out=h_w[:].bitcast(E5M2), scales=h_s[:], in_=hid[:].rearrange("p o t -> p (o t)")
+        )
+        for h in range(2):
+            cols = slice(h * P, (h + 1) * P)
+            nc.tensor.matmul_mx(
+                out=p_ps[h][:],
+                lhsT=wb_w[:, cols].bitcast(E4M3),
+                lhsT_scale=wb_s[:, cols],
+                rhs=h_w[:].bitcast(E5M2),
+                rhs_scale=h_s[:],
+                start=False,
+                stop=True,
+            )
+        p_sb = [keep.tile([P, O], F32, name="p_sb%d" % h) for h in range(2)]
+        nc.scalar.copy(p_sb[0][:], p_ps[0][:])
+        nc.scalar.activation(pages[0][:].indirect(l7[:]), p_sb[0][:], COPY)
+        nc.scalar.dma_start(out=out[0:P, :], in_=pages[0][:])
+        nc.vector.tensor_copy(p_sb[1][:], p_ps[1][:])
+        nc.vector.tensor_copy(pages[1][:].indirect(l7[:]), p_sb[1][:])
+        nc.sync.dma_start(out=out[P : 2 * P, :], in_=pages[1][:])

@@ -69,14 +69,14 @@ def tile_list_ownladder_chosen_further_scattered_kernel(
         for t in range(PACK):
             nc.vector.memset(pw[t][:], 0.0)
 
-        nc.sync.dma_start(l1[:], offs)
-        load_scale_rows(nc.scalar, wt_s, wt_scales)
         nc.sync.dma_start(out=xt_w[:].bitcast(I32), in_=xt_words[0].bitcast(I32))
         nc.sync.dma_start(l2[:], offs2)
+        nc.sync.dma_start(l1[:], offs)
+        load_scale_rows(nc.sync, wt_s, wt_scales)
         nc.sync.dma_start(
             out=wt_w[:].bitcast(I32), in_=wt_words[0].rearrange("p n t -> p (n t)").bitcast(I32)
         )
-        load_scale_rows(nc.scalar, xt_s, xt_scales)
+        load_scale_rows(nc.sync, xt_s, xt_scales)
         nc.sync.dma_start(l3[:], offs3)
         nc.sync.dma_start(out=sa_t[:], in_=sa.rearrange("(p t) o -> p (t o)", t=PACK))
         nc.sync.dma_start(l4[:], offs4)
@@ -92,115 +92,141 @@ def tile_list_ownladder_chosen_further_scattered_kernel(
         load_scale_rows(nc.sync, wb_s, wb_scales)
         nc.sync.dma_start(l7[:], offs7)
 
-        g_ws = keep.tile([P, PACK, P], U8, name="g_ws", align_bytes=64)
-        g_ww = keep.tile([P, PACK, P], U32, name="g_ww", align_bytes=64)
-        x2_w = keep.tile([P, J], U16, name="x2_w", align_bytes=64)
-        x2_s = keep.tile([P, J], U8, name="x2_s", align_bytes=64)
+        g_ws = keep.tile([P, PACK, P], U8, name="g_ws", tag="slot1", align_bytes=64)
+        g_ww = keep.tile([P, PACK, P], U32, name="g_ww", tag="slot0", align_bytes=64)
+        x2_w = keep.tile([P, J], U16, name="x2_w", tag="x_w", align_bytes=64)
+        x2_s = keep.tile([P, J], U8, name="x2_s", tag="x_s", align_bytes=64)
+        first, second = slice(0, P), slice(P, 2 * P)
+        first_e, second_e = slice(0, P // 16), slice(P // 16, 2 * P // 16)
+        nc.vector.tensor_copy(x2_w[:, first], xt_w[:].indirect(l2[:, first_e]))
         nc.vector.tensor_copy(g_ws[:].rearrange("p t m -> p m t"), wt_s[:].indirect(l1[:]))
-        nc.vector.tensor_copy(x2_w[:], xt_w[:].indirect(l2[:]))
         nc.vector.tensor_copy(g_ww[:].rearrange("p t m -> p m t"), wt_w[:].indirect(l1[:]))
-        nc.vector.tensor_copy(x2_s[:], xt_s[:].indirect(l2[:]))
+        nc.vector.tensor_copy(x2_s[:, first], xt_s[:].indirect(l2[:, first_e]))
+        nc.vector.tensor_copy(x2_w[:, second], xt_w[:].indirect(l2[:, second_e]))
+        nc.vector.tensor_copy(x2_s[:, second], xt_s[:].indirect(l2[:, second_e]))
 
-        a_sb = []
-        for t in range(PACK):
-            acc = psum.tile([P, J], F32, name="a_ps%d" % t)
+        def hidden(acc, t, cols):
             nc.tensor.matmul_mx(
-                out=acc[:],
+                out=acc,
                 lhsT=g_ww[:, t, :].bitcast(E5M2),
                 lhsT_scale=g_ws[:, t, :],
-                rhs=x2_w[:].bitcast(E2M1),
-                rhs_scale=x2_s[:],
+                rhs=x2_w[:, cols].bitcast(E2M1),
+                rhs_scale=x2_s[:, cols],
                 start=True,
                 stop=True,
             )
-            a_t = keep.tile([P, J], F32, name="a_sb%d" % t, tag="slot%d" % t)
-            if t == 0:
-                nc.scalar.copy(a_t[:], acc[:])
-            else:
-                nc.vector.tensor_copy(a_t[:], acc[:])
-            a_sb.append(a_t)
 
-        x6_w = keep.tile([P, O], U16, name="x6_w", align_bytes=64)
-        x6_s = keep.tile([P, O], U8, name="x6_s", align_bytes=64)
-        nc.vector.tensor_copy(x6_w[:], xt_w[:].indirect(l6[:]))
-        nc.vector.tensor_copy(x6_s[:], xt_s[:].indirect(l6[:]))
-        p_ps = [psum.tile([P, O], F32, name="p_ps%d" % h) for h in range(2)]
-        for h in range(2):
-            cols = slice(h * P, (h + 1) * P)
-            nc.tensor.matmul_mx(
-                out=p_ps[h][:],
-                lhsT=ws_w[:, cols].bitcast(E4M3),
-                lhsT_scale=ws_s[:, cols],
-                rhs=x6_w[:].bitcast(E2M1),
-                rhs_scale=x6_s[:],
-                start=True,
-                stop=False,
-            )
+        ps0 = psum.tile([P, P], F32, name="ps0")
+        ps1 = psum.tile([P, P], F32, name="ps1")
+        ps01 = psum.tile([P, 2, P], F32, name="ps01")
+        ps23 = psum.tile([P, 2, J], F32, name="ps23")
+        a0 = keep.tile([P, P], F32, name="a0")
+        a1 = keep.tile([P, P], F32, name="a1")
+        a01 = keep.tile([P, 2, P], F32, name="a01")
+        a23 = keep.tile([P, 2, J], F32, name="a23")
+        hidden(ps0[:], 0, first)
+        nc.scalar.copy(a0[:], ps0[:])
+        hidden(ps1[:], 1, first)
+        nc.vector.tensor_copy(a1[:], ps1[:])
+        hidden(ps01[:, 0, :], 0, second)
+        hidden(ps01[:, 1, :], 1, second)
+        nc.vector.tensor_copy(a01[:], ps01[:])
+        hidden(ps23[:, 0, :], 2, slice(0, J))
+        hidden(ps23[:, 1, :], 3, slice(0, J))
+        nc.vector.tensor_copy(a23[:], ps23[:])
 
-        hid = keep.tile([P, O, PACK], BF16, name="hid", align_bytes=64)
+        hid = [keep.tile([P, P, PACK], BF16, name="hid%d" % u, align_bytes=64) for u in range(2)]
         looked = [keep.tile([P, C], F32, name="looked%d" % t) for t in range(PACK)]
         pg = [keep.tile([P, C], F32, name="pg%d" % t) for t in range(PACK)]
 
-        def place(t):
-            nc.scalar.activation(pw[t][:].indirect(l3[:]), a_sb[t][:], COPY)
+        def place(t, values, entries):
+            nc.scalar.activation(pw[t][:].indirect(l3[:, entries]), values, COPY)
 
-        def look(t, u):
-            cols = slice(u * HALF, (u + 1) * HALF)
-            entries = slice(u * HALF // 16, (u + 1) * HALF // 16)
+        def look(t, c0, c1):
+            cols = slice(c0, c1)
+            entries = slice(c0 // 16, c1 // 16)
             nc.scalar.activation(
                 looked[t][:, cols], pw[t][:].indirect(l4[:, entries]), COPY, scale=sa_t[:, t : t + 1]
             )
             nc.vector.tensor_tensor(pg[t][:, cols], pw[t][:, cols], looked[t][:, cols], MAX)
 
         def pick(t):
-            nc.vector.tensor_copy(hid[:, :, t], pg[t][:].indirect(l5[:]))
+            nc.vector.tensor_copy(hid[0][:, :, t], pg[t][:].indirect(l5[:, first_e]))
+            nc.vector.tensor_copy(hid[1][:, :, t], pg[t][:].indirect(l5[:, second_e]))
 
         pages = []
 
         def clear_page(h):
-            page = keep.tile([P, E], F32, name="page%d" % h, tag="slot%d" % h)
+            page = keep.tile([P, E], F32, name="page%d" % h, tag="slot%d" % h, align_bytes=64)
             nc.vector.memset(page[:], 0.0)
             pages.append(page)
 
-        place(0)
-        place(1)
-        look(0, 0)
-        look(0, 1)
+        whole = slice(0, J // 16)
+        place(0, a0[:], first_e)
+        place(1, a1[:], first_e)
+        place(0, a01[:, 0, :], second_e)
+        place(1, a01[:, 1, :], second_e)
+        look(0, 0, 256)
+        look(0, 256, 512)
         pick(0)
+        place(2, a23[:, 0, :], whole)
+
+        x6_w = keep.tile([P, O], U16, name="x6_w", tag="x_w", align_bytes=64)
+        x6_s = keep.tile([P, O], U8, name="x6_s", tag="x_s", align_bytes=64)
+        nc.vector.tensor_copy(x6_w[:], xt_w[:].indirect(l6[:]))
+        nc.vector.tensor_copy(x6_s[:], xt_s[:].indirect(l6[:]))
+        p_ps = [[psum.tile([P, P], F32, name="p_ps%d%d" % (h, u)) for u in range(2)] for h in range(2)]
+        halves = (first, second)
+        for u in range(2):
+            for h in range(2):
+                nc.tensor.matmul_mx(
+                    out=p_ps[h][u][:],
+                    lhsT=ws_w[:, halves[h]].bitcast(E4M3),
+                    lhsT_scale=ws_s[:, halves[h]],
+                    rhs=x6_w[:, halves[u]].bitcast(E2M1),
+                    rhs_scale=x6_s[:, halves[u]],
+                    start=True,
+                    stop=False,
+                )
         clear_page(0)
-        place(2)
-        look(1, 0)
-        look(1, 1)
-        pick(1)
         clear_page(1)
-        look(2, 0)
-        place(3)
-        look(2, 1)
+
+        look(1, 0, 256)
+        look(1, 256, 512)
+        pick(1)
+        look(2, 0, 256)
+        look(2, 256, 512)
         pick(2)
-        look(3, 0)
-        look(3, 1)
+        place(3, a23[:, 1, :], whole)
+        look(3, 0, 256)
+        look(3, 256, 416)
+        look(3, 416, 512)
         pick(3)
 
-        h_w = keep.tile([P, O], U32, name="h_w", align_bytes=64)
-        h_s = keep.tile([P, O], U8, name="h_s", align_bytes=64)
-        nc.vector.quantize_mx(
-            out=h_w[:].bitcast(E5M2), scales=h_s[:], in_=hid[:].rearrange("p o t -> p (o t)")
-        )
-        for h in range(2):
-            cols = slice(h * P, (h + 1) * P)
-            nc.tensor.matmul_mx(
-                out=p_ps[h][:],
-                lhsT=wb_w[:, cols].bitcast(E4M3),
-                lhsT_scale=wb_s[:, cols],
-                rhs=h_w[:].bitcast(E5M2),
-                rhs_scale=h_s[:],
-                start=False,
-                stop=True,
-            )
         p_sb = [keep.tile([P, O], F32, name="p_sb%d" % h) for h in range(2)]
-        nc.scalar.copy(p_sb[0][:], p_ps[0][:])
-        nc.scalar.activation(pages[0][:].indirect(l7[:]), p_sb[0][:], COPY)
+        for u in range(2):
+            h_w = keep.tile([P, P], U32, name="h_w%d" % u, align_bytes=64)
+            h_s = keep.tile([P, P], U8, name="h_s%d" % u, align_bytes=64)
+            nc.vector.quantize_mx(
+                out=h_w[:].bitcast(E5M2), scales=h_s[:], in_=hid[u][:].rearrange("p o t -> p (o t)")
+            )
+            for h in range(2):
+                nc.tensor.matmul_mx(
+                    out=p_ps[h][u][:],
+                    lhsT=wb_w[:, halves[h]].bitcast(E4M3),
+                    lhsT_scale=wb_s[:, halves[h]],
+                    rhs=h_w[:].bitcast(E5M2),
+                    rhs_scale=h_s[:],
+                    start=False,
+                    stop=True,
+                )
+        p0b = keep.tile([P, P], F32, name="p0b")
+        nc.scalar.copy(p_sb[0][:, first], p_ps[0][0][:])
+        nc.scalar.activation(pages[0][:].indirect(l7[:, first_e]), p_sb[0][:, first], COPY)
+        nc.vector.tensor_copy(p_sb[1][:, first], p_ps[1][0][:])
+        nc.vector.tensor_copy(p0b[:], p_ps[0][1][:])
+        nc.scalar.activation(pages[0][:].indirect(l7[:, second_e]), p0b[:], COPY)
         nc.scalar.dma_start(out=out[0:P, :], in_=pages[0][:])
-        nc.vector.tensor_copy(p_sb[1][:], p_ps[1][:])
+        nc.vector.tensor_copy(p_sb[1][:, second], p_ps[1][1][:])
         nc.vector.tensor_copy(pages[1][:].indirect(l7[:]), p_sb[1][:])
         nc.sync.dma_start(out=out[P : 2 * P, :], in_=pages[1][:])

@@ -226,7 +226,7 @@ def tile_list_ownladder_chosen_further_scattered_kernel(
         nc.vector.tensor_copy(p_sb[1][:, first], p_ps[1][0][:])
         nc.vector.tensor_copy(p0b[:], p_ps[0][1][:])
         nc.scalar.activation(pages[0][:].indirect(l7[:, second_e]), p0b[:], COPY)
-        nc.scalar.dma_start(out=out[0:P, :], in_=pages[0][:])
+        nc.sync.dma_start(out=out[0:P, :], in_=pages[0][:])
         nc.vector.tensor_copy(p_sb[1][:, second], p_ps[1][1][:])
         nc.vector.tensor_copy(pages[1][:].indirect(l7[:]), p_sb[1][:])
         nc.sync.dma_start(out=out[P : 2 * P, :], in_=pages[1][:])

from contextlib import ExitStack

import concourse.mybir as mybir

K, T, J, R, V, C, O, N, E = 512, 1024, 256, 512, 1024, 512, 256, 256, 1024
FLOPS = 2 * K * R * J + 2 * R * N * O + 2 * K * N * O

F32 = mybir.dt.float32
BF16 = mybir.dt.bfloat16
I32 = mybir.dt.int32
U32 = mybir.dt.uint32
U16 = mybir.dt.uint16
U8 = mybir.dt.uint8
E4M3 = mybir.dt.float8_e4m3fn_x4
E5M2 = mybir.dt.float8_e5m2_x4
E2M1 = mybir.dt.float4_e2m1fn_x4
COPY = mybir.ActivationFunctionType.Copy
MAX = mybir.AluOpType.max

P = 128
PACK = 4
HALF = C // 2


def load_scale_rows(queue, plane, scales):
    for q in range(4):
        queue.dma_start(
            out=plane[32 * q : 32 * q + 4, :].bitcast(I32),
            in_=scales[0, 4 * q : 4 * q + 4, :].bitcast(I32),
        )


def tile_list_ownladder_chosen_further_scattered_kernel(
    tc, xt_words, xt_scales, wt_words, wt_scales, sa, wb_words, wb_scales, ws_words, ws_scales,
    offs, offs2, offs3, offs4, offs5, offs6, offs7, out,
):
    nc = tc.nc
    with ExitStack() as ctx:
        lists = ctx.enter_context(tc.tile_pool(name="lists", bufs=1))
        keep = ctx.enter_context(tc.tile_pool(name="keep", bufs=1))
        psum = ctx.enter_context(tc.psum_pool(name="psum", bufs=1))

        def list_tile(name, entries):
            return lists.tile([P, entries // 16], U16, name=name)

        l1 = list_tile("l1", R)
        l2 = list_tile("l2", J)
        l3 = list_tile("l3", J)
        l4 = list_tile("l4", C)
        l5 = list_tile("l5", O)
        l6 = list_tile("l6", O)
        l7 = list_tile("l7", O)

        wt_w = keep.tile([P, V], U32, name="wt_w", align_bytes=64)
        wt_s = keep.tile([P, V], U8, name="wt_s", align_bytes=64)
        xt_w = keep.tile([P, T], U16, name="xt_w", align_bytes=64)
        xt_s = keep.tile([P, T], U8, name="xt_s", align_bytes=64)
        wb_w = keep.tile([P, N], U32, name="wb_w", align_bytes=64)
        wb_s = keep.tile([P, N], U8, name="wb_s", align_bytes=64)
        ws_w = keep.tile([P, N], U32, name="ws_w", align_bytes=64)
        ws_s = keep.tile([P, N], U8, name="ws_s", align_bytes=64)
        sa_t = keep.tile([P, PACK], F32, name="sa_t")
        pw = [keep.tile([P, C], F32, name="pw%d" % t) for t in range(PACK)]

        nc.vector.memset(wt_s[:].bitcast(I32), 0)
        nc.vector.memset(xt_s[:].bitcast(I32), 0)
        nc.vector.memset(ws_s[:].bitcast(I32), 0)
        nc.vector.memset(wb_s[:].bitcast(I32), 0)
        for t in range(PACK):
            nc.vector.memset(pw[t][:], 0.0)

        nc.sync.dma_start(out=xt_w[:].bitcast(I32), in_=xt_words[0].bitcast(I32))
        nc.sync.dma_start(l2[:], offs2)
        nc.sync.dma_start(l1[:], offs)
        load_scale_rows(nc.sync, wt_s, wt_scales)
        nc.sync.dma_start(
            out=wt_w[:].bitcast(I32), in_=wt_words[0].rearrange("p n t -> p (n t)").bitcast(I32)
        )
        load_scale_rows(nc.sync, xt_s, xt_scales)
        nc.sync.dma_start(l3[:], offs3)
        nc.sync.dma_start(out=sa_t[:], in_=sa.rearrange("(p t) o -> p (t o)", t=PACK))
        nc.sync.dma_start(l4[:], offs4)
        nc.sync.dma_start(l6[:], offs6)
        nc.sync.dma_start(l5[:], offs5)
        nc.sync.dma_start(
            out=ws_w[:].bitcast(I32), in_=ws_words[0].rearrange("p n t -> p (n t)").bitcast(I32)
        )
        load_scale_rows(nc.sync, ws_s, ws_scales)
        nc.sync.dma_start(
            out=wb_w[:].bitcast(I32), in_=wb_words[0].rearrange("p n t -> p (n t)").bitcast(I32)
        )
        load_scale_rows(nc.sync, wb_s, wb_scales)
        nc.sync.dma_start(l7[:], offs7)

        g_ws = keep.tile([P, PACK, P], U8, name="g_ws", tag="slot1", align_bytes=64)
        g_ww = keep.tile([P, PACK, P], U32, name="g_ww", tag="slot0", align_bytes=64)
        x2_w = keep.tile([P, J], U16, name="x2_w", tag="x_w", align_bytes=64)
        x2_s = keep.tile([P, J], U8, name="x2_s", tag="x_s", align_bytes=64)
        first, second = slice(0, P), slice(P, 2 * P)
        first_e, second_e = slice(0, P // 16), slice(P // 16, 2 * P // 16)
        nc.vector.tensor_copy(x2_w[:, first], xt_w[:].indirect(l2[:, first_e]))
        nc.vector.tensor_copy(g_ws[:].rearrange("p t m -> p m t"), wt_s[:].indirect(l1[:]))
        nc.vector.tensor_copy(g_ww[:].rearrange("p t m -> p m t"), wt_w[:].indirect(l1[:]))
        nc.vector.tensor_copy(x2_s[:, first], xt_s[:].indirect(l2[:, first_e]))
        nc.vector.tensor_copy(x2_w[:, second], xt_w[:].indirect(l2[:, second_e]))
        nc.vector.tensor_copy(x2_s[:, second], xt_s[:].indirect(l2[:, second_e]))

        def hidden(acc, t, cols):
            nc.tensor.matmul_mx(
                out=acc,
                lhsT=g_ww[:, t, :].bitcast(E5M2),
                lhsT_scale=g_ws[:, t, :],
                rhs=x2_w[:, cols].bitcast(E2M1),
                rhs_scale=x2_s[:, cols],
                start=True,
                stop=True,
            )

        ps0 = psum.tile([P, P], F32, name="ps0")
        ps1 = psum.tile([P, P], F32, name="ps1")
        ps01 = psum.tile([P, 2, P], F32, name="ps01")
        ps23 = psum.tile([P, 2, J], F32, name="ps23")
        a0 = keep.tile([P, P], F32, name="a0")
        a1 = keep.tile([P, P], F32, name="a1")
        a01 = keep.tile([P, 2, P], F32, name="a01")
        a23 = keep.tile([P, 2, J], F32, name="a23")
        hidden(ps0[:], 0, first)
        nc.scalar.copy(a0[:], ps0[:])
        hidden(ps1[:], 1, first)
        nc.vector.tensor_copy(a1[:], ps1[:])
        hidden(ps01[:, 0, :], 0, second)
        hidden(ps01[:, 1, :], 1, second)
        nc.vector.tensor_copy(a01[:], ps01[:])
        hidden(ps23[:, 0, :], 2, slice(0, J))
        hidden(ps23[:, 1, :], 3, slice(0, J))
        nc.vector.tensor_copy(a23[:], ps23[:])

        hid = [keep.tile([P, P, PACK], BF16, name="hid%d" % u, align_bytes=64) for u in range(2)]
        looked = [keep.tile([P, C], F32, name="looked%d" % t) for t in range(PACK)]
        pg = [keep.tile([P, C], F32, name="pg%d" % t) for t in range(PACK)]

        def place(t, values, entries):
            nc.scalar.activation(pw[t][:].indirect(l3[:, entries]), values, COPY)

        def look(t, c0, c1):
            cols = slice(c0, c1)
            entries = slice(c0 // 16, c1 // 16)
            nc.scalar.activation(
                looked[t][:, cols], pw[t][:].indirect(l4[:, entries]), COPY, scale=sa_t[:, t : t + 1]
            )
            nc.vector.tensor_tensor(pg[t][:, cols], pw[t][:, cols], looked[t][:, cols], MAX)

        def pick(t):
            nc.vector.tensor_copy(hid[0][:, :, t], pg[t][:].indirect(l5[:, first_e]))
            nc.vector.tensor_copy(hid[1][:, :, t], pg[t][:].indirect(l5[:, second_e]))

        pages = []

        def clear_page(h):
            page = keep.tile([P, E], F32, name="page%d" % h, tag="slot%d" % h, align_bytes=64)
            nc.vector.memset(page[:], 0.0)
            pages.append(page)

        whole = slice(0, J // 16)
        place(0, a0[:], first_e)
        place(1, a1[:], first_e)
        place(0, a01[:, 0, :], second_e)
        place(1, a01[:, 1, :], second_e)
        look(0, 0, 256)
        look(0, 256, 512)
        pick(0)
        place(2, a23[:, 0, :], whole)

        x6_w = keep.tile([P, O], U16, name="x6_w", tag="x_w", align_bytes=64)
        x6_s = keep.tile([P, O], U8, name="x6_s", tag="x_s", align_bytes=64)
        nc.vector.tensor_copy(x6_w[:], xt_w[:].indirect(l6[:]))
        nc.vector.tensor_copy(x6_s[:], xt_s[:].indirect(l6[:]))
        p_ps = [[psum.tile([P, P], F32, name="p_ps%d%d" % (h, u)) for u in range(2)] for h in range(2)]
        halves = (first, second)
        for u in range(2):
            for h in range(2):
                nc.tensor.matmul_mx(
                    out=p_ps[h][u][:],
                    lhsT=ws_w[:, halves[h]].bitcast(E4M3),
                    lhsT_scale=ws_s[:, halves[h]],
                    rhs=x6_w[:, halves[u]].bitcast(E2M1),
                    rhs_scale=x6_s[:, halves[u]],
                    start=True,
                    stop=False,
                )
        clear_page(0)
        clear_page(1)

        look(1, 0, 256)
        look(1, 256, 512)
        pick(1)
        look(2, 0, 256)
        look(2, 256, 512)
        pick(2)
        place(3, a23[:, 1, :], whole)
        look(3, 0, 256)
        look(3, 256, 416)
        look(3, 416, 512)
        pick(3)

        p_sb = [keep.tile([P, O], F32, name="p_sb%d" % h) for h in range(2)]
        for u in range(2):
            h_w = keep.tile([P, P], U32, name="h_w%d" % u, align_bytes=64)
            h_s = keep.tile([P, P], U8, name="h_s%d" % u, align_bytes=64)
            nc.vector.quantize_mx(
                out=h_w[:].bitcast(E5M2), scales=h_s[:], in_=hid[u][:].rearrange("p o t -> p (o t)")
            )
            for h in range(2):
                nc.tensor.matmul_mx(
                    out=p_ps[h][u][:],
                    lhsT=wb_w[:, halves[h]].bitcast(E4M3),
                    lhsT_scale=wb_s[:, halves[h]],
                    rhs=h_w[:].bitcast(E5M2),
                    rhs_scale=h_s[:],
                    start=False,
                    stop=True,
                )
        p0b = keep.tile([P, P], F32, name="p0b")
        nc.scalar.copy(p_sb[0][:, first], p_ps[0][0][:])
        nc.scalar.activation(pages[0][:].indirect(l7[:, first_e]), p_sb[0][:, first], COPY)
        nc.vector.tensor_copy(p_sb[1][:, first], p_ps[1][0][:])
        nc.vector.tensor_copy(p0b[:], p_ps[0][1][:])
        nc.scalar.activation(pages[0][:].indirect(l7[:, second_e]), p0b[:], COPY)
        nc.sync.dma_start(out=out[0:P, :], in_=pages[0][:])
        nc.vector.tensor_copy(p_sb[1][:, second], p_ps[1][1][:])
        nc.vector.tensor_copy(pages[1][:].indirect(l7[:]), p_sb[1][:])
        nc.sync.dma_start(out=out[P : 2 * P, :], in_=pages[1][:])
